import numpy as np
import ml_dtypes


def mxq(x, axis, fmt="e4m3"):
    dtype, down = {"e4m3": (ml_dtypes.float8_e4m3fn, 7), "e5m2": (ml_dtypes.float8_e5m2, 14)}[fmt]
    v = np.moveaxis(np.asarray(x, np.float32).astype(ml_dtypes.bfloat16).astype(np.float64), axis, -1)
    blocks = v.reshape(v.shape[:-1] + (-1, 32))
    amax = np.abs(blocks).max(-1, keepdims=True)
    byte = np.maximum(np.where(amax > 0, np.frexp(amax)[1] - 1 + 127, 0) - down, 1)
    scale = np.exp2(byte - 127.0)
    codes = (blocks / scale).astype(np.float32).astype(dtype).astype(np.float64)
    return np.moveaxis((codes * scale).reshape(v.shape), -1, axis)


WIDE = False


def mx_kscale(k):
    if not WIDE:
        return np.ones(k)
    levels = np.array([30, -30])
    if k % 512:
        return np.exp2(np.random.permutation(np.resize(levels, k // 32))).repeat(32)
    a = np.empty((k // 512, 16))
    for p in range(k // 512):
        a[p, :8] = np.random.permutation(np.resize(levels, 8))
        for g in range(8):
            far = levels[np.abs(levels - a[p, g]) >= 10]
            a[p, g + 8] = far[np.random.randint(len(far))]
    return np.exp2(a.ravel()).repeat(32)


def f64(x):
    return np.asarray(x).astype(np.float64)


def striped(idx):
    return np.tile(np.asarray(idx).reshape(-1, 16).T, (8, 1)).astype(np.uint16)


def unstriped(offs):
    return offs[:16].T.reshape(-1).astype(np.int64)


E2M1 = np.array([0.0, 0.5, 1.0, 1.5, 2.0, 3.0, 4.0, 6.0, -0.0, -0.5, -1.0, -1.5, -2.0, -3.0, -4.0, -6.0])


def pack_weight(w, fmt):
    k, n = w.shape
    w = f64(np.asarray(w, np.float32).astype(ml_dtypes.bfloat16)).reshape(k // 32, 32, n)
    amax = np.abs(w).max(1)
    if fmt in ("e4m3", "e5m2"):
        byte = np.frexp(amax)[1] - 1 + 127 - (7 if fmt == "e4m3" else 14)
    else:
        mant, ex = np.frexp(amax / 6.0)
        byte = np.where(mant > 0.5, ex, ex - 1) + 127
    byte = np.clip(np.where(amax > 0, byte, 1), 1, 254)
    scaled = (w * np.exp2(127.0 - byte)[:, None, :]).reshape(k, n).astype(np.float32)
    by_word = np.ascontiguousarray(scaled.reshape(k // 512, 128, 4, n).transpose(0, 1, 3, 2))
    if fmt in ("e4m3", "e5m2"):
        words = by_word.astype(ml_dtypes.float8_e4m3fn if fmt == "e4m3" else ml_dtypes.float8_e5m2).view(np.uint8)
    else:
        c = by_word.astype(ml_dtypes.float4_e2m1fn).view(np.uint8) & 0xF
        words = (c[..., 0::2] | (c[..., 1::2] << 4)).reshape(k // 512, 128, 2 * n)
    return np.ascontiguousarray(words), np.ascontiguousarray(byte.astype(np.uint8).reshape(k // 512, 16, n))


def unpack_weight(words, scales, fmt):
    g, _, n = scales.shape
    words = np.ascontiguousarray(words).reshape(g, 128, n, -1)
    if fmt in ("e4m3", "e5m2"):
        vals = words.view(ml_dtypes.float8_e4m3fn if fmt == "e4m3" else ml_dtypes.float8_e5m2).astype(np.float64)
    else:
        nib = np.empty((g, 128, n, 4), np.uint8)
        nib[..., 0::2] = words & 0xF
        nib[..., 1::2] = words >> 4
        vals = E2M1[nib]
    vals = vals * np.repeat(np.exp2(scales.astype(np.float64) - 127.0), 8, axis=1)[..., None]
    return vals.transpose(0, 1, 3, 2).reshape(g * 512, n)


K, T, J, S, R, V, N = 1024, 1024, 256, 512, 512, 512, 256


def setup_inputs():
    n = np.random.standard_normal
    idx = np.random.permutation(T)[:J]
    idx2 = np.random.permutation(S)[:J]
    idx3 = np.random.permutation(V)[:J]
    fk = mx_kscale(K)
    fr = mx_kscale(R)
    wp = pack_weight(n((K, R)) * 1 / np.sqrt(K) * fk[:, None] * fr, "e5m2")
    wbp = pack_weight(n((R, N)) * 1 / np.sqrt(R) / fr[:, None], "e2m1")
    return {
        "xa": (n((K, T))).astype(np.float32),
        "xb": (n((K, S))).astype(np.float32),
        "fk": (np.random.uniform(0.5, 2.0, (K, 1)) / fk[:, None]).astype(np.float32),
        "w_words": wp[0],
        "w_scales": wp[1],
        "tb": (n((R, V)) * 0.7 * fr[:, None]).astype(np.float32),
        "wb_words": wbp[0],
        "wb_scales": wbp[1],
        "rs": (1.0 * n((J, N))).astype(np.float32),
        "offs": striped(idx),
        "offs2": striped(idx2),
        "offs3": striped(idx3),
    }


def reference(xa, xb, fk, w_words, w_scales, tb, wb_words, wb_scales, rs, offs, offs2, offs3):
    idx = unstriped(offs)
    idx2 = unstriped(offs2)
    idx3 = unstriped(offs3)
    wu = unpack_weight(w_words, w_scales, "e5m2")
    wbu = unpack_weight(wb_words, wb_scales, "e2m1")
    u = f64(xa)[:, idx] * f64(xb)[:, idx2] * f64(fk)
    uq = mxq(u, 0, "e5m2")
    a = wu.T @ uq
    hid = np.maximum(a, f64(tb)[:, idx3])
    hidq = mxq(hid, 0, "e5m2")
    p = hidq.T @ wbu
    pk2 = np.max(np.abs(p), axis=1, keepdims=True)
    y = p / (pk2 + 0.2) + 0.3 * f64(rs)
    return y

@@ -1,0 +1,171 @@
+from contextlib import ExitStack
+
+import concourse.mybir as mybir
+
+K, T, J, S, R, V, N = 1024, 1024, 256, 512, 512, 512, 256
+FLOPS = 2 * K * R * J + 2 * R * J * N
+
+F32 = mybir.dt.float32
+BF16 = mybir.dt.bfloat16
+I32 = mybir.dt.int32
+U32 = mybir.dt.uint32
+U16 = mybir.dt.uint16
+U8 = mybir.dt.uint8
+E5M2X4 = mybir.dt.float8_e5m2_x4
+E2M1X4 = mybir.dt.float4_e2m1fn_x4
+ALU = mybir.AluOpType
+ACT = mybir.ActivationFunctionType
+
+P = 128
+PACK = 4
+PASSES = K // (P * PACK)
+HALVES = J // P
+LIST_COLS = J // 16
+
+
+def tile_list_entryproducts_abovetable_rowpeaks_kernel(
+    tc, xa, xb, fk, w_words, w_scales, tb, wb_words, wb_scales, rs, offs, offs2, offs3, out
+):
+    nc = tc.nc
+    with ExitStack() as ctx:
+        sb = ctx.enter_context(tc.tile_pool(name="sb", bufs=1))
+        ps = ctx.enter_context(tc.psum_pool(name="ps", bufs=1))
+
+        def tile(shape, dtype, name):
+            return sb.tile(shape, dtype, name=name, align_bytes=64)
+
+        list_a = tile([P, LIST_COLS], U16, "list_a")
+        list_b = tile([P, LIST_COLS], U16, "list_b")
+        list_t = tile([P, LIST_COLS], U16, "list_t")
+        w_raw = tile([P, PASSES, R], I32, "w_raw")
+        xb_rows = [tile([P, PACK, S], F32, f"xb_rows{a}") for a in range(PASSES)]
+        xa_rows = [[tile([P, T], F32, f"xa_rows{a}{t}") for t in range(PACK)] for a in range(PASSES)]
+        tb_rows = [tile([P, V], F32, f"tb_rows{t}") for t in range(PACK)]
+        wb_codes = tile([P, 2 * N], U8, "wb_codes")
+        rs_rows = tile([P, HALVES, N], F32, "rs_rows")
+        fk_cols = tile([P, PASSES, PACK], F32, "fk_cols")
+        w_sc_raw = tile([P, PASSES, R], U8, "w_sc_raw")
+        wb_sc = tile([P, N], U8, "wb_sc")
+
+        xa_v = xa.rearrange("(a p t) c -> a t p c", a=PASSES, t=PACK)
+        xb_v = xb.rearrange("(a p t) c -> a p t c", a=PASSES, t=PACK)
+        tb_v = tb.rearrange("(p t) c -> t p c", t=PACK)
+
+        nc.vector.memset(w_sc_raw[:].bitcast(I32), 0)
+        nc.gpsimd.memset(wb_sc[:].bitcast(I32), 0)
+        nc.sync.dma_start(out=w_raw[:], in_=w_words.rearrange("a p c t -> p a (c t)").bitcast(I32))
+        nc.sync.dma_start(list_b[:], offs2)
+        nc.sync.dma_start(out=xb_rows[0][:], in_=xb_v[0])
+        nc.sync.dma_start(list_a[:], offs)
+        nc.scalar.dma_start(out=fk_cols[:], in_=fk.rearrange("(a p t) o -> p a (t o)", a=PASSES, t=PACK))
+        for q in range(4):
+            nc.scalar.dma_start(
+                out=w_sc_raw[32 * q : 32 * q + 4, :, :].bitcast(I32),
+                in_=w_scales[:, 4 * q : 4 * q + 4, :].rearrange("a r c -> r a c").bitcast(I32),
+            )
+        for t in range(PACK):
+            nc.sync.dma_start(out=xa_rows[0][t][:], in_=xa_v[0, t])
+        nc.sync.dma_start(list_t[:], offs3)
+        nc.sync.dma_start(out=xb_rows[1][:], in_=xb_v[1])
+        for t in range(PACK):
+            nc.sync.dma_start(out=xa_rows[1][t][:], in_=xa_v[1, t])
+        for t in range(PACK):
+            nc.sync.dma_start(out=tb_rows[t][:], in_=tb_v[t])
+        nc.sync.dma_start(out=wb_codes[:].bitcast(I32), in_=wb_words[0].bitcast(I32))
+        nc.sync.dma_start(out=rs_rows[:], in_=rs.rearrange("(h p) n -> p h n", p=P))
+
+        for q in range(4):
+            nc.gpsimd.dma_start(
+                out=wb_sc[32 * q : 32 * q + 4, :].bitcast(I32),
+                in_=wb_scales[0, 4 * q : 4 * q + 4, :].bitcast(I32),
+            )
+
+        w_codes = tile([P, PACK, PASSES, P], U32, "w_codes")
+        w_sc = tile([P, PACK, PASSES, P], U8, "w_sc")
+        nc.vector.tensor_copy(
+            out=w_codes[:].rearrange("p t a (c i) -> p a c t i", i=4),
+            in_=w_raw[:].bitcast(U32).rearrange("p a (c i t) -> p a c t i", i=4, t=PACK),
+        )
+
+        acc = [ps.tile([P, PACK, P], F32, name=f"acc{h}") for h in range(HALVES)]
+        for a in range(PASSES):
+            prod = tile([P, PACK, J], F32, f"prod{a}")
+            for t in range(PACK):
+                b_scaled = tile([P, J], F32, f"b_scaled{a}{t}")
+                b_picked = tile([P, J], F32, f"b_picked{a}{t}")
+                nc.scalar.activation(b_picked[:], xb_rows[a][:, t, :].indirect(list_b[:]), ACT.Copy)
+                nc.scalar.activation(b_scaled[:], b_picked[:], ACT.Copy, scale=fk_cols[:, a, t : t + 1])
+                nc.vector.tensor_tensor(prod[:, t, :], xa_rows[a][t][:].indirect(list_a[:]), b_scaled[:], ALU.mult)
+            if a == 0:
+                nc.vector.tensor_copy(
+                    out=w_sc[:].rearrange("p t a (c i) -> p a c t i", i=16),
+                    in_=w_sc_raw[:].rearrange("p a (c i t) -> p a c t i", i=16, t=PACK),
+                )
+            u_bf = [tile([P, P * PACK], BF16, f"u_bf{a}{h}") for h in range(HALVES)]
+            u_codes = [tile([P, P], U32, f"u_codes{a}{h}") for h in range(HALVES)]
+            u_sc = [tile([P, P], U8, f"u_sc{a}{h}") for h in range(HALVES)]
+            for h in range(HALVES):
+                nc.vector.tensor_copy(
+                    out=u_bf[h][:].rearrange("p (c i t) -> p c t i", i=4, t=PACK),
+                    in_=prod[:, :, h * P : (h + 1) * P].rearrange("p t (c i) -> p c t i", i=4),
+                )
+            for h in range(HALVES):
+                nc.vector.quantize_mx(out=u_codes[h][:].bitcast(E5M2X4), scales=u_sc[h][:], in_=u_bf[h][:])
+            for h in range(HALVES):
+                for t in range(PACK):
+                    nc.tensor.matmul_mx(
+                        out=acc[h][:, t, :],
+                        lhsT=w_codes[:, t, a, :].bitcast(E5M2X4),
+                        lhsT_scale=w_sc[:, t, a, :],
+                        rhs=u_codes[h][:].bitcast(E5M2X4),
+                        rhs_scale=u_sc[h][:],
+                        start=(a == 0 and t == 0),
+                        stop=(a == PASSES - 1 and t == PACK - 1),
+                    )
+
+        tb_picked = [tile([P, PACK, P], F32, f"tb_picked{h}") for h in range(HALVES)]
+        half_cols = LIST_COLS // HALVES
+        for t in range(PACK):
+            for h in range(HALVES):
+                nc.scalar.activation(
+                    tb_picked[h][:, t, :],
+                    tb_rows[t][:].indirect(list_t[:, h * half_cols : (h + 1) * half_cols]),
+                    ACT.Copy,
+                )
+        rs_scaled = tile([P, HALVES, N], F32, "rs_scaled")
+        nc.scalar.activation(rs_scaled[:], rs_rows[:], ACT.Copy, scale=0.3)
+
+        hid_bf = [tile([P, P * PACK], BF16, f"hid_bf{h}") for h in range(HALVES)]
+        hid_codes = [tile([P, P], U32, f"hid_codes{h}") for h in range(HALVES)]
+        hid_sc = [tile([P, P], U8, f"hid_sc{h}") for h in range(HALVES)]
+        for h in range(HALVES):
+            nc.vector.tensor_tensor(
+                hid_bf[h][:].rearrange("p (c i t) -> p c t i", i=4, t=PACK),
+                acc[h][:].rearrange("p t (c i) -> p c t i", i=4),
+                tb_picked[h][:].rearrange("p t (c i) -> p c t i", i=4),
+                ALU.max,
+            )
+        p_acc = [ps.tile([P, N], F32, name=f"p_acc{h}") for h in range(HALVES)]
+        p_abs = [tile([P, N], F32, f"p_abs{h}") for h in range(HALVES)]
+        for h in range(HALVES):
+            nc.vector.quantize_mx(out=hid_codes[h][:].bitcast(E5M2X4), scales=hid_sc[h][:], in_=hid_bf[h][:])
+            nc.tensor.matmul_mx(
+                out=p_acc[h][:],
+                lhsT=hid_codes[h][:].bitcast(E5M2X4),
+                lhsT_scale=hid_sc[h][:],
+                rhs=wb_codes[:].bitcast(E2M1X4),
+                rhs_scale=wb_sc[:],
+                start=True,
+                stop=True,
+            )
+            nc.scalar.activation(p_abs[h][:], p_acc[h][:], ACT.Abs)
+        out_v = out.rearrange("(h p) n -> h p n", p=P)
+        for h in range(HALVES):
+            shifted = tile([P, N], F32, f"shifted{h}")
+            den = tile([P, 1], F32, f"den{h}")
+            inv = tile([P, 1], F32, f"inv{h}")
+            y = tile([P, N], F32, f"y{h}")
+            nc.vector.tensor_scalar(shifted[:], p_abs[h][:], 0.2, None, ALU.add, ALU.max, accum_out=den[:])
+            nc.vector.reciprocal(inv[:], den[:])
+            nc.vector.scalar_tensor_tensor(y[:], p_acc[h][:], inv[:], rs_scaled[:, h, :], ALU.mult, ALU.add)
+            nc.sync.dma_start(out=out_v[h], in_=y[:])

@@ -39,7 +39,12 @@ def tile_list_entryproducts_abovetable_rowpeaks_kernel(
         list_t = tile([P, LIST_COLS], U16, "list_t")
         w_raw = tile([P, PASSES, R], I32, "w_raw")
         xb_rows = [tile([P, PACK, S], F32, f"xb_rows{a}") for a in range(PASSES)]
-        xa_rows = [[tile([P, T], F32, f"xa_rows{a}{t}") for t in range(PACK)] for a in range(PASSES)]
+        xa_cuts = [[(0, 2), (2, 4)], [(0, 2), (2, 3), (3, 4)]]
+        xa_rows = [[tile([P, hi - lo, T], F32, f"xa_rows{a}{lo}") for lo, hi in xa_cuts[a]] for a in range(PASSES)]
+        xa_plane = [
+            [xa_rows[a][n][:, t - lo, :] for n, (lo, hi) in enumerate(xa_cuts[a]) for t in range(lo, hi)]
+            for a in range(PASSES)
+        ]
         tb_rows = [tile([P, V], F32, f"tb_rows{t}") for t in range(PACK)]
         wb_codes = tile([P, 2 * N], U8, "wb_codes")
         rs_rows = tile([P, HALVES, N], F32, "rs_rows")
@@ -47,7 +52,7 @@ def tile_list_entryproducts_abovetable_rowpeaks_kernel(
         w_sc_raw = tile([P, PASSES, R], U8, "w_sc_raw")
         wb_sc = tile([P, N], U8, "wb_sc")
 
-        xa_v = xa.rearrange("(a p t) c -> a t p c", a=PASSES, t=PACK)
+        xa_v = xa.rearrange("(a p t) c -> a p t c", a=PASSES, t=PACK)
         xb_v = xb.rearrange("(a p t) c -> a p t c", a=PASSES, t=PACK)
         tb_v = tb.rearrange("(p t) c -> t p c", t=PACK)
 
@@ -55,20 +60,20 @@ def tile_list_entryproducts_abovetable_rowpeaks_kernel(
         nc.gpsimd.memset(wb_sc[:].bitcast(I32), 0)
         nc.sync.dma_start(out=w_raw[:], in_=w_words.rearrange("a p c t -> p a (c t)").bitcast(I32))
         nc.sync.dma_start(list_b[:], offs2)
-        nc.sync.dma_start(out=xb_rows[0][:], in_=xb_v[0])
-        nc.sync.dma_start(list_a[:], offs)
         nc.scalar.dma_start(out=fk_cols[:], in_=fk.rearrange("(a p t) o -> p a (t o)", a=PASSES, t=PACK))
         for q in range(4):
             nc.scalar.dma_start(
                 out=w_sc_raw[32 * q : 32 * q + 4, :, :].bitcast(I32),
                 in_=w_scales[:, 4 * q : 4 * q + 4, :].rearrange("a r c -> r a c").bitcast(I32),
             )
-        for t in range(PACK):
-            nc.sync.dma_start(out=xa_rows[0][t][:], in_=xa_v[0, t])
-        nc.sync.dma_start(list_t[:], offs3)
-        nc.sync.dma_start(out=xb_rows[1][:], in_=xb_v[1])
-        for t in range(PACK):
-            nc.sync.dma_start(out=xa_rows[1][t][:], in_=xa_v[1, t])
+        for a in range(PASSES):
+            nc.sync.dma_start(out=xb_rows[a][:], in_=xb_v[a])
+            if a == 0:
+                nc.sync.dma_start(list_a[:], offs)
+            else:
+                nc.sync.dma_start(list_t[:], offs3)
+            for n, (lo, hi) in enumerate(xa_cuts[a]):
+                nc.sync.dma_start(out=xa_rows[a][n][:], in_=xa_v[a, :, lo:hi, :])
         for t in range(PACK):
             nc.sync.dma_start(out=tb_rows[t][:], in_=tb_v[t])
         nc.sync.dma_start(out=wb_codes[:].bitcast(I32), in_=wb_words[0].bitcast(I32))
@@ -86,28 +91,40 @@ def tile_list_entryproducts_abovetable_rowpeaks_kernel(
             out=w_codes[:].rearrange("p t a (c i) -> p a c t i", i=4),
             in_=w_raw[:].bitcast(U32).rearrange("p a (c i t) -> p a c t i", i=4, t=PACK),
         )
+        nc.vector.tensor_copy(
+            out=w_sc[:].rearrange("p t a (c i) -> p a c t i", i=16),
+            in_=w_sc_raw[:].rearrange("p a (c i t) -> p a c t i", i=16, t=PACK),
+        )
 
+        half_cols = LIST_COLS // HALVES
         acc = [ps.tile([P, PACK, P], F32, name=f"acc{h}") for h in range(HALVES)]
         for a in range(PASSES):
-            prod = tile([P, PACK, J], F32, f"prod{a}")
+            prod = tile([P, HALVES, PACK, P], F32, f"prod{a}")
+            b_picked = [tile([P, HALVES, P], F32, f"b_picked{a}{t}") for t in range(PACK)]
             for t in range(PACK):
-                b_scaled = tile([P, J], F32, f"b_scaled{a}{t}")
-                b_picked = tile([P, J], F32, f"b_picked{a}{t}")
-                nc.scalar.activation(b_picked[:], xb_rows[a][:, t, :].indirect(list_b[:]), ACT.Copy)
-                nc.scalar.activation(b_scaled[:], b_picked[:], ACT.Copy, scale=fk_cols[:, a, t : t + 1])
-                nc.vector.tensor_tensor(prod[:, t, :], xa_rows[a][t][:].indirect(list_a[:]), b_scaled[:], ALU.mult)
-            if a == 0:
-                nc.vector.tensor_copy(
-                    out=w_sc[:].rearrange("p t a (c i) -> p a c t i", i=16),
-                    in_=w_sc_raw[:].rearrange("p a (c i t) -> p a c t i", i=16, t=PACK),
+                nc.scalar.activation(
+                    b_picked[t][:].rearrange("p h j -> p (h j)"), xb_rows[a][:, t, :].indirect(list_b[:]), ACT.Copy
                 )
+            for t in range(PACK):
+                a_picked = tile([P, HALVES, P], F32, f"a_picked{a}{t}")
+                nc.vector.tensor_copy(a_picked[:, 0, :], xa_plane[a][t].indirect(list_a[:, 0:half_cols]))
+                nc.scalar.activation(a_picked[:, 1, :], xa_plane[a][t].indirect(list_a[:, half_cols:LIST_COLS]), ACT.Copy)
+                for hs in [slice(0, 1), slice(1, 2)] if t == PACK - 1 else [slice(0, HALVES)]:
+                    nc.vector.scalar_tensor_tensor(
+                        prod[:, hs, t, :],
+                        a_picked[:, hs, :],
+                        fk_cols[:, a, t : t + 1],
+                        b_picked[t][:, hs, :],
+                        ALU.mult,
+                        ALU.mult,
+                    )
             u_bf = [tile([P, P * PACK], BF16, f"u_bf{a}{h}") for h in range(HALVES)]
             u_codes = [tile([P, P], U32, f"u_codes{a}{h}") for h in range(HALVES)]
             u_sc = [tile([P, P], U8, f"u_sc{a}{h}") for h in range(HALVES)]
             for h in range(HALVES):
                 nc.vector.tensor_copy(
                     out=u_bf[h][:].rearrange("p (c i t) -> p c t i", i=4, t=PACK),
-                    in_=prod[:, :, h * P : (h + 1) * P].rearrange("p t (c i) -> p c t i", i=4),
+                    in_=prod[:, h, :, :].rearrange("p t (c i) -> p c t i", i=4),
                 )
             for h in range(HALVES):
                 nc.vector.quantize_mx(out=u_codes[h][:].bitcast(E5M2X4), scales=u_sc[h][:], in_=u_bf[h][:])
@@ -123,15 +140,9 @@ def tile_list_entryproducts_abovetable_rowpeaks_kernel(
                         stop=(a == PASSES - 1 and t == PACK - 1),
                     )
 
-        tb_picked = [tile([P, PACK, P], F32, f"tb_picked{h}") for h in range(HALVES)]
-        half_cols = LIST_COLS // HALVES
+        tb_picked = tile([P, PACK, J], F32, "tb_picked")
         for t in range(PACK):
-            for h in range(HALVES):
-                nc.scalar.activation(
-                    tb_picked[h][:, t, :],
-                    tb_rows[t][:].indirect(list_t[:, h * half_cols : (h + 1) * half_cols]),
-                    ACT.Copy,
-                )
+            nc.scalar.activation(tb_picked[:, t, :], tb_rows[t][:].indirect(list_t[:]), ACT.Copy)
         rs_scaled = tile([P, HALVES, N], F32, "rs_scaled")
         nc.scalar.activation(rs_scaled[:], rs_rows[:], ACT.Copy, scale=0.3)
 
@@ -142,7 +153,7 @@ def tile_list_entryproducts_abovetable_rowpeaks_kernel(
             nc.vector.tensor_tensor(
                 hid_bf[h][:].rearrange("p (c i t) -> p c t i", i=4, t=PACK),
                 acc[h][:].rearrange("p t (c i) -> p c t i", i=4),
-                tb_picked[h][:].rearrange("p t (c i) -> p c t i", i=4),
+                tb_picked[:, :, h * P : (h + 1) * P].rearrange("p t (c i) -> p c t i", i=4),
                 ALU.max,
             )
         p_acc = [ps.tile([P, N], F32, name=f"p_acc{h}") for h in range(HALVES)]

@@ -39,7 +39,7 @@ def tile_list_entryproducts_abovetable_rowpeaks_kernel(
         list_t = tile([P, LIST_COLS], U16, "list_t")
         w_raw = tile([P, PASSES, R], I32, "w_raw")
         xb_rows = [tile([P, PACK, S], F32, f"xb_rows{a}") for a in range(PASSES)]
-        xa_cuts = [[(0, 2), (2, 4)], [(0, 2), (2, 3), (3, 4)]]
+        xa_cuts = [[(0, 4)], [(0, 2), (2, 3), (3, 4)]]
         xa_rows = [[tile([P, hi - lo, T], F32, f"xa_rows{a}{lo}") for lo, hi in xa_cuts[a]] for a in range(PASSES)]
         xa_plane = [
             [xa_rows[a][n][:, t - lo, :] for n, (lo, hi) in enumerate(xa_cuts[a]) for t in range(lo, hi)]
@@ -57,7 +57,7 @@ def tile_list_entryproducts_abovetable_rowpeaks_kernel(
         tb_v = tb.rearrange("(p t) c -> t p c", t=PACK)
 
         nc.vector.memset(w_sc_raw[:].bitcast(I32), 0)
-        nc.gpsimd.memset(wb_sc[:].bitcast(I32), 0)
+        nc.vector.memset(wb_sc[:].bitcast(I32), 0)
         nc.sync.dma_start(out=w_raw[:], in_=w_words.rearrange("a p c t -> p a (c t)").bitcast(I32))
         nc.sync.dma_start(list_b[:], offs2)
         nc.scalar.dma_start(out=fk_cols[:], in_=fk.rearrange("(a p t) o -> p a (t o)", a=PASSES, t=PACK))
@@ -80,7 +80,7 @@ def tile_list_entryproducts_abovetable_rowpeaks_kernel(
         nc.sync.dma_start(out=rs_rows[:], in_=rs.rearrange("(h p) n -> p h n", p=P))
 
         for q in range(4):
-            nc.gpsimd.dma_start(
+            nc.sync.dma_start(
                 out=wb_sc[32 * q : 32 * q + 4, :].bitcast(I32),
                 in_=wb_scales[0, 4 * q : 4 * q + 4, :].bitcast(I32),
             )
@@ -141,8 +141,14 @@ def tile_list_entryproducts_abovetable_rowpeaks_kernel(
                     )
 
         tb_picked = tile([P, PACK, J], F32, "tb_picked")
-        for t in range(PACK):
+        for t in range(PACK - 1):
             nc.scalar.activation(tb_picked[:, t, :], tb_rows[t][:].indirect(list_t[:]), ACT.Copy)
+        for h in range(HALVES):
+            nc.scalar.activation(
+                tb_picked[:, PACK - 1, h * P : (h + 1) * P],
+                tb_rows[PACK - 1][:].indirect(list_t[:, h * half_cols : (h + 1) * half_cols]),
+                ACT.Copy,
+            )
         rs_scaled = tile([P, HALVES, N], F32, "rs_scaled")
         nc.scalar.activation(rs_scaled[:], rs_rows[:], ACT.Copy, scale=0.3)
 
@@ -171,12 +177,14 @@ def tile_list_entryproducts_abovetable_rowpeaks_kernel(
             )
             nc.scalar.activation(p_abs[h][:], p_acc[h][:], ACT.Abs)
         out_v = out.rearrange("(h p) n -> h p n", p=P)
+        shifted = [tile([P, N], F32, f"shifted{h}") for h in range(HALVES)]
+        den = [tile([P, 1], F32, f"den{h}") for h in range(HALVES)]
+        inv = [tile([P, 1], F32, f"inv{h}") for h in range(HALVES)]
+        y = [tile([P, N], F32, f"y{h}") for h in range(HALVES)]
         for h in range(HALVES):
-            shifted = tile([P, N], F32, f"shifted{h}")
-            den = tile([P, 1], F32, f"den{h}")
-            inv = tile([P, 1], F32, f"inv{h}")
-            y = tile([P, N], F32, f"y{h}")
-            nc.vector.tensor_scalar(shifted[:], p_abs[h][:], 0.2, None, ALU.add, ALU.max, accum_out=den[:])
-            nc.vector.reciprocal(inv[:], den[:])
-            nc.vector.scalar_tensor_tensor(y[:], p_acc[h][:], inv[:], rs_scaled[:, h, :], ALU.mult, ALU.add)
-            nc.sync.dma_start(out=out_v[h], in_=y[:])
+            nc.vector.tensor_scalar(shifted[h][:], p_abs[h][:], 0.2, None, ALU.add, ALU.max, accum_out=den[h][:])
+        for h in range(HALVES):
+            nc.vector.reciprocal(inv[h][:], den[h][:])
+        for h in range(HALVES):
+            nc.vector.scalar_tensor_tensor(y[h][:], p_acc[h][:], inv[h][:], rs_scaled[:, h, :], ALU.mult, ALU.add)
+            nc.sync.dma_start(out=out_v[h], in_=y[h][:])

@@ -34,6 +34,12 @@ def tile_list_entryproducts_abovetable_rowpeaks_kernel(
         def tile(shape, dtype, name):
             return sb.tile(shape, dtype, name=name, align_bytes=64)
 
+        def pick_on_vector(picked, window, offsets):
+            nc.vector.tensor_copy(picked, window.indirect(offsets))
+
+        def pick_on_scalar(picked, window, offsets):
+            nc.scalar.activation(picked, window.indirect(offsets), ACT.Copy)
+
         list_a = tile([P, LIST_COLS], U16, "list_a")
         list_b = tile([P, LIST_COLS], U16, "list_b")
         list_t = tile([P, LIST_COLS], U16, "list_t")
@@ -48,7 +54,7 @@ def tile_list_entryproducts_abovetable_rowpeaks_kernel(
         tb_rows = [tile([P, V], F32, f"tb_rows{t}") for t in range(PACK)]
         wb_codes = tile([P, 2 * N], U8, "wb_codes")
         rs_rows = tile([P, HALVES, N], F32, "rs_rows")
-        fk_cols = tile([P, PASSES, PACK], F32, "fk_cols")
+        fk_cols = tile([P, PASSES, 2 * PACK], F32, "fk_cols")
         w_sc_raw = tile([P, PASSES, R], U8, "w_sc_raw")
         wb_sc = tile([P, N], U8, "wb_sc")
 
@@ -59,8 +65,7 @@ def tile_list_entryproducts_abovetable_rowpeaks_kernel(
         nc.vector.memset(w_sc_raw[:].bitcast(I32), 0)
         nc.vector.memset(wb_sc[:].bitcast(I32), 0)
         nc.sync.dma_start(out=w_raw[:], in_=w_words.rearrange("a p c t -> p a (c t)").bitcast(I32))
-        nc.sync.dma_start(list_b[:], offs2)
-        nc.scalar.dma_start(out=fk_cols[:], in_=fk.rearrange("(a p t) o -> p a (t o)", a=PASSES, t=PACK))
+        nc.scalar.dma_start(out=fk_cols[:, :, 0:PACK], in_=fk.rearrange("(a p t) o -> p a (t o)", a=PASSES, t=PACK))
         for q in range(4):
             nc.scalar.dma_start(
                 out=w_sc_raw[32 * q : 32 * q + 4, :, :].bitcast(I32),
@@ -69,11 +74,12 @@ def tile_list_entryproducts_abovetable_rowpeaks_kernel(
         for a in range(PASSES):
             nc.sync.dma_start(out=xb_rows[a][:], in_=xb_v[a])
             if a == 0:
-                nc.sync.dma_start(list_a[:], offs)
-            else:
-                nc.sync.dma_start(list_t[:], offs3)
+                nc.sync.dma_start(list_b[:], offs2)
             for n, (lo, hi) in enumerate(xa_cuts[a]):
                 nc.sync.dma_start(out=xa_rows[a][n][:], in_=xa_v[a, :, lo:hi, :])
+            if a == 0:
+                nc.sync.dma_start(list_a[:], offs)
+        nc.sync.dma_start(list_t[:], offs3)
         for t in range(PACK):
             nc.sync.dma_start(out=tb_rows[t][:], in_=tb_v[t])
         nc.sync.dma_start(out=wb_codes[:].bitcast(I32), in_=wb_words[0].bitcast(I32))
@@ -101,14 +107,18 @@ def tile_list_entryproducts_abovetable_rowpeaks_kernel(
         for a in range(PASSES):
             prod = tile([P, HALVES, PACK, P], F32, f"prod{a}")
             b_picked = [tile([P, HALVES, P], F32, f"b_picked{a}{t}") for t in range(PACK)]
+            last_pass = a == PASSES - 1
             for t in range(PACK):
-                nc.scalar.activation(
-                    b_picked[t][:].rearrange("p h j -> p (h j)"), xb_rows[a][:, t, :].indirect(list_b[:]), ACT.Copy
-                )
+                pick = pick_on_vector if last_pass and t == PACK - 1 else pick_on_scalar
+                pick(b_picked[t][:].rearrange("p h j -> p (h j)"), xb_rows[a][:, t, :], list_b[:])
             for t in range(PACK):
                 a_picked = tile([P, HALVES, P], F32, f"a_picked{a}{t}")
-                nc.vector.tensor_copy(a_picked[:, 0, :], xa_plane[a][t].indirect(list_a[:, 0:half_cols]))
-                nc.scalar.activation(a_picked[:, 1, :], xa_plane[a][t].indirect(list_a[:, half_cols:LIST_COLS]), ACT.Copy)
+                if last_pass and t == PACK - 1:
+                    pick_on_vector(a_picked[:, 0, :], xa_plane[a][t], list_a[:, 0:half_cols])
+                    pick_on_scalar(a_picked[:, 1, :], xa_plane[a][t], list_a[:, half_cols:LIST_COLS])
+                else:
+                    pick = pick_on_vector if t == 0 else pick_on_scalar
+                    pick(a_picked[:].rearrange("p h j -> p (h j)"), xa_plane[a][t], list_a[:])
                 for hs in [slice(0, 1), slice(1, 2)] if t == PACK - 1 else [slice(0, HALVES)]:
                     nc.vector.scalar_tensor_tensor(
                         prod[:, hs, t, :],

from contextlib import ExitStack

import concourse.mybir as mybir

K, T, J, S, R, V, N = 1024, 1024, 256, 512, 512, 512, 256
FLOPS = 2 * K * R * J + 2 * R * J * N

F32 = mybir.dt.float32
BF16 = mybir.dt.bfloat16
I32 = mybir.dt.int32
U32 = mybir.dt.uint32
U16 = mybir.dt.uint16
U8 = mybir.dt.uint8
E5M2X4 = mybir.dt.float8_e5m2_x4
E2M1X4 = mybir.dt.float4_e2m1fn_x4
ALU = mybir.AluOpType
ACT = mybir.ActivationFunctionType

P = 128
PACK = 4
PASSES = K // (P * PACK)
HALVES = J // P
LIST_COLS = J // 16


def tile_list_entryproducts_abovetable_rowpeaks_kernel(
    tc, xa, xb, fk, w_words, w_scales, tb, wb_words, wb_scales, rs, offs, offs2, offs3, out
):
    nc = tc.nc
    with ExitStack() as ctx:
        sb = ctx.enter_context(tc.tile_pool(name="sb", bufs=1))
        ps = ctx.enter_context(tc.psum_pool(name="ps", bufs=1))

        def tile(shape, dtype, name):
            return sb.tile(shape, dtype, name=name, align_bytes=64)

        def pick_on_vector(picked, window, offsets):
            nc.vector.tensor_copy(picked, window.indirect(offsets))

        def pick_on_scalar(picked, window, offsets):
            nc.scalar.activation(picked, window.indirect(offsets), ACT.Copy)

        list_a = tile([P, LIST_COLS], U16, "list_a")
        list_b = tile([P, LIST_COLS], U16, "list_b")
        list_t = tile([P, LIST_COLS], U16, "list_t")
        w_raw = tile([P, PASSES, R], I32, "w_raw")
        xb_rows = [tile([P, PACK, S], F32, f"xb_rows{a}") for a in range(PASSES)]
        xa_cuts = [[(0, 4)], [(0, 2), (2, 3), (3, 4)]]
        xa_rows = [[tile([P, hi - lo, T], F32, f"xa_rows{a}{lo}") for lo, hi in xa_cuts[a]] for a in range(PASSES)]
        xa_plane = [
            [xa_rows[a][n][:, t - lo, :] for n, (lo, hi) in enumerate(xa_cuts[a]) for t in range(lo, hi)]
            for a in range(PASSES)
        ]
        tb_rows = [tile([P, V], F32, f"tb_rows{t}") for t in range(PACK)]
        wb_codes = tile([P, 2 * N], U8, "wb_codes")
        rs_rows = tile([P, HALVES, N], F32, "rs_rows")
        fk_cols = tile([P, PASSES, 2 * PACK], F32, "fk_cols")
        w_sc_raw = tile([P, PASSES, R], U8, "w_sc_raw")
        wb_sc = tile([P, N], U8, "wb_sc")

        xa_v = xa.rearrange("(a p t) c -> a p t c", a=PASSES, t=PACK)
        xb_v = xb.rearrange("(a p t) c -> a p t c", a=PASSES, t=PACK)
        tb_v = tb.rearrange("(p t) c -> t p c", t=PACK)

        nc.vector.memset(w_sc_raw[:].bitcast(I32), 0)
        nc.vector.memset(wb_sc[:].bitcast(I32), 0)
        nc.sync.dma_start(out=w_raw[:], in_=w_words.rearrange("a p c t -> p a (c t)").bitcast(I32))
        nc.scalar.dma_start(out=fk_cols[:, :, 0:PACK], in_=fk.rearrange("(a p t) o -> p a (t o)", a=PASSES, t=PACK))
        for q in range(4):
            nc.scalar.dma_start(
                out=w_sc_raw[32 * q : 32 * q + 4, :, :].bitcast(I32),
                in_=w_scales[:, 4 * q : 4 * q + 4, :].rearrange("a r c -> r a c").bitcast(I32),
            )
        for a in range(PASSES):
            nc.sync.dma_start(out=xb_rows[a][:], in_=xb_v[a])
            if a == 0:
                nc.sync.dma_start(list_b[:], offs2)
            for n, (lo, hi) in enumerate(xa_cuts[a]):
                nc.sync.dma_start(out=xa_rows[a][n][:], in_=xa_v[a, :, lo:hi, :])
            if a == 0:
                nc.sync.dma_start(list_a[:], offs)
        nc.sync.dma_start(list_t[:], offs3)
        for t in range(PACK):
            nc.sync.dma_start(out=tb_rows[t][:], in_=tb_v[t])
        nc.sync.dma_start(out=wb_codes[:].bitcast(I32), in_=wb_words[0].bitcast(I32))
        nc.sync.dma_start(out=rs_rows[:], in_=rs.rearrange("(h p) n -> p h n", p=P))

        for q in range(4):
            nc.sync.dma_start(
                out=wb_sc[32 * q : 32 * q + 4, :].bitcast(I32),
                in_=wb_scales[0, 4 * q : 4 * q + 4, :].bitcast(I32),
            )

        w_codes = tile([P, PACK, PASSES, P], U32, "w_codes")
        w_sc = tile([P, PACK, PASSES, P], U8, "w_sc")
        nc.vector.tensor_copy(
            out=w_codes[:].rearrange("p t a (c i) -> p a c t i", i=4),
            in_=w_raw[:].bitcast(U32).rearrange("p a (c i t) -> p a c t i", i=4, t=PACK),
        )
        nc.vector.tensor_copy(
            out=w_sc[:].rearrange("p t a (c i) -> p a c t i", i=16),
            in_=w_sc_raw[:].rearrange("p a (c i t) -> p a c t i", i=16, t=PACK),
        )

        half_cols = LIST_COLS // HALVES
        acc = [ps.tile([P, PACK, P], F32, name=f"acc{h}") for h in range(HALVES)]
        for a in range(PASSES):
            prod = tile([P, HALVES, PACK, P], F32, f"prod{a}")
            b_picked = [tile([P, HALVES, P], F32, f"b_picked{a}{t}") for t in range(PACK)]
            last_pass = a == PASSES - 1
            for t in range(PACK):
                pick = pick_on_vector if last_pass and t == PACK - 1 else pick_on_scalar
                pick(b_picked[t][:].rearrange("p h j -> p (h j)"), xb_rows[a][:, t, :], list_b[:])
            for t in range(PACK):
                a_picked = tile([P, HALVES, P], F32, f"a_picked{a}{t}")
                if last_pass and t == PACK - 1:
                    pick_on_vector(a_picked[:, 0, :], xa_plane[a][t], list_a[:, 0:half_cols])
                    pick_on_scalar(a_picked[:, 1, :], xa_plane[a][t], list_a[:, half_cols:LIST_COLS])
                else:
                    pick = pick_on_vector if t == 0 else pick_on_scalar
                    pick(a_picked[:].rearrange("p h j -> p (h j)"), xa_plane[a][t], list_a[:])
                for hs in [slice(0, 1), slice(1, 2)] if t == PACK - 1 else [slice(0, HALVES)]:
                    nc.vector.scalar_tensor_tensor(
                        prod[:, hs, t, :],
                        a_picked[:, hs, :],
                        fk_cols[:, a, t : t + 1],
                        b_picked[t][:, hs, :],
                        ALU.mult,
                        ALU.mult,
                    )
            u_bf = [tile([P, P * PACK], BF16, f"u_bf{a}{h}") for h in range(HALVES)]
            u_codes = [tile([P, P], U32, f"u_codes{a}{h}") for h in range(HALVES)]
            u_sc = [tile([P, P], U8, f"u_sc{a}{h}") for h in range(HALVES)]
            for h in range(HALVES):
                nc.vector.tensor_copy(
                    out=u_bf[h][:].rearrange("p (c i t) -> p c t i", i=4, t=PACK),
                    in_=prod[:, h, :, :].rearrange("p t (c i) -> p c t i", i=4),
                )
            for h in range(HALVES):
                nc.vector.quantize_mx(out=u_codes[h][:].bitcast(E5M2X4), scales=u_sc[h][:], in_=u_bf[h][:])
            for h in range(HALVES):
                for t in range(PACK):
                    nc.tensor.matmul_mx(
                        out=acc[h][:, t, :],
                        lhsT=w_codes[:, t, a, :].bitcast(E5M2X4),
                        lhsT_scale=w_sc[:, t, a, :],
                        rhs=u_codes[h][:].bitcast(E5M2X4),
                        rhs_scale=u_sc[h][:],
                        start=(a == 0 and t == 0),
                        stop=(a == PASSES - 1 and t == PACK - 1),
                    )

        tb_picked = tile([P, PACK, J], F32, "tb_picked")
        for t in range(PACK - 1):
            nc.scalar.activation(tb_picked[:, t, :], tb_rows[t][:].indirect(list_t[:]), ACT.Copy)
        for h in range(HALVES):
            nc.scalar.activation(
                tb_picked[:, PACK - 1, h * P : (h + 1) * P],
                tb_rows[PACK - 1][:].indirect(list_t[:, h * half_cols : (h + 1) * half_cols]),
                ACT.Copy,
            )
        rs_scaled = tile([P, HALVES, N], F32, "rs_scaled")
        nc.scalar.activation(rs_scaled[:], rs_rows[:], ACT.Copy, scale=0.3)

        hid_bf = [tile([P, P * PACK], BF16, f"hid_bf{h}") for h in range(HALVES)]
        hid_codes = [tile([P, P], U32, f"hid_codes{h}") for h in range(HALVES)]
        hid_sc = [tile([P, P], U8, f"hid_sc{h}") for h in range(HALVES)]
        for h in range(HALVES):
            nc.vector.tensor_tensor(
                hid_bf[h][:].rearrange("p (c i t) -> p c t i", i=4, t=PACK),
                acc[h][:].rearrange("p t (c i) -> p c t i", i=4),
                tb_picked[:, :, h * P : (h + 1) * P].rearrange("p t (c i) -> p c t i", i=4),
                ALU.max,
            )
        p_acc = [ps.tile([P, N], F32, name=f"p_acc{h}") for h in range(HALVES)]
        p_abs = [tile([P, N], F32, f"p_abs{h}") for h in range(HALVES)]
        for h in range(HALVES):
            nc.vector.quantize_mx(out=hid_codes[h][:].bitcast(E5M2X4), scales=hid_sc[h][:], in_=hid_bf[h][:])
            nc.tensor.matmul_mx(
                out=p_acc[h][:],
                lhsT=hid_codes[h][:].bitcast(E5M2X4),
                lhsT_scale=hid_sc[h][:],
                rhs=wb_codes[:].bitcast(E2M1X4),
                rhs_scale=wb_sc[:],
                start=True,
                stop=True,
            )
            nc.scalar.activation(p_abs[h][:], p_acc[h][:], ACT.Abs)
        out_v = out.rearrange("(h p) n -> h p n", p=P)
        shifted = [tile([P, N], F32, f"shifted{h}") for h in range(HALVES)]
        den = [tile([P, 1], F32, f"den{h}") for h in range(HALVES)]
        inv = [tile([P, 1], F32, f"inv{h}") for h in range(HALVES)]
        y = [tile([P, N], F32, f"y{h}") for h in range(HALVES)]
        for h in range(HALVES):
            nc.vector.tensor_scalar(shifted[h][:], p_abs[h][:], 0.2, None, ALU.add, ALU.max, accum_out=den[h][:])
        for h in range(HALVES):
            nc.vector.reciprocal(inv[h][:], den[h][:])
        for h in range(HALVES):
            nc.vector.scalar_tensor_tensor(y[h][:], p_acc[h][:], inv[h][:], rs_scaled[:, h, :], ALU.mult, ALU.add)
            nc.sync.dma_start(out=out_v[h], in_=y[h][:])
